import numpy as np
import ml_dtypes


def mxq(x, axis, fmt="e4m3"):
    dtype, down = {"e4m3": (ml_dtypes.float8_e4m3fn, 7), "e5m2": (ml_dtypes.float8_e5m2, 14)}[fmt]
    v = np.moveaxis(np.asarray(x, np.float32).astype(ml_dtypes.bfloat16).astype(np.float64), axis, -1)
    blocks = v.reshape(v.shape[:-1] + (-1, 32))
    amax = np.abs(blocks).max(-1, keepdims=True)
    byte = np.maximum(np.where(amax > 0, np.frexp(amax)[1] - 1 + 127, 0) - down, 1)
    scale = np.exp2(byte - 127.0)
    codes = (blocks / scale).astype(np.float32).astype(dtype).astype(np.float64)
    return np.moveaxis((codes * scale).reshape(v.shape), -1, axis)


WIDE = False


def mx_kscale(k):
    if not WIDE:
        return np.ones(k)
    levels = np.array([30, -30])
    if k % 512:
        return np.exp2(np.random.permutation(np.resize(levels, k // 32))).repeat(32)
    a = np.empty((k // 512, 16))
    for p in range(k // 512):
        a[p, :8] = np.random.permutation(np.resize(levels, 8))
        for g in range(8):
            far = levels[np.abs(levels - a[p, g]) >= 10]
            a[p, g + 8] = far[np.random.randint(len(far))]
    return np.exp2(a.ravel()).repeat(32)


def f64(x):
    return np.asarray(x).astype(np.float64)


E2M1 = np.array([0.0, 0.5, 1.0, 1.5, 2.0, 3.0, 4.0, 6.0, -0.0, -0.5, -1.0, -1.5, -2.0, -3.0, -4.0, -6.0])


def pack_weight(w, fmt):
    k, n = w.shape
    w = f64(np.asarray(w, np.float32).astype(ml_dtypes.bfloat16)).reshape(k // 32, 32, n)
    amax = np.abs(w).max(1)
    if fmt == "e4m3":
        byte = np.frexp(amax)[1] - 1 + 127 - 7
    else:
        mant, ex = np.frexp(amax / 6.0)
        byte = np.where(mant > 0.5, ex, ex - 1) + 127
    byte = np.clip(np.where(amax > 0, byte, 1), 1, 254)
    scaled = (w * np.exp2(127.0 - byte)[:, None, :]).reshape(k, n).astype(np.float32)
    by_word = np.ascontiguousarray(scaled.reshape(k // 512, 128, 4, n).transpose(0, 1, 3, 2))
    if fmt == "e4m3":
        words = by_word.astype(ml_dtypes.float8_e4m3fn).view(np.uint8)
    else:
        c = by_word.astype(ml_dtypes.float4_e2m1fn).view(np.uint8) & 0xF
        words = (c[..., 0::2] | (c[..., 1::2] << 4)).reshape(k // 512, 128, 2 * n)
    return np.ascontiguousarray(words), np.ascontiguousarray(byte.astype(np.uint8).reshape(k // 512, 16, n))


def unpack_weight(words, scales, fmt):
    g, _, n = scales.shape
    words = np.ascontiguousarray(words).reshape(g, 128, n, -1)
    if fmt == "e4m3":
        vals = words.view(ml_dtypes.float8_e4m3fn).astype(np.float64)
    else:
        nib = np.empty((g, 128, n, 4), np.uint8)
        nib[..., 0::2] = words & 0xF
        nib[..., 1::2] = words >> 4
        vals = E2M1[nib]
    vals = vals * np.repeat(np.exp2(scales.astype(np.float64) - 127.0), 8, axis=1)[..., None]
    return vals.transpose(0, 1, 3, 2).reshape(g * 512, n)


def bf(x):
    return np.asarray(x, np.float32).astype(ml_dtypes.bfloat16)


def planes(Y):
    r, m = Y.shape
    b = f64(bf(Y)).reshape(r // 32, 32, m)
    amax = np.abs(b).max(1)
    byte = np.clip(np.where(amax > 0, np.frexp(amax)[1] - 1 + 127 - 7, 1), 1, 254)
    codes = (b * np.exp2(127.0 - byte)[:, None, :]).reshape(r, m).astype(np.float32).astype(ml_dtypes.float8_e4m3fn).view(np.uint8)
    words = codes.reshape(r // 512, 128, 4, m).transpose(0, 1, 3, 2)
    return np.ascontiguousarray(words), np.ascontiguousarray(byte.astype(np.uint8).reshape(r // 512, 16, m))


K, N, T, S = 512, 512, 1024, 1024


def setup_inputs():
    n = np.random.standard_normal
    ft = mx_kscale(T)
    fs = mx_kscale(S)
    sap = pack_weight(n((S, K)) * fs[:, None], "e2m1")
    sbp = pack_weight(n((S, N)) / fs[:, None], "e4m3")
    return {
        "xa": (n((K, T))).astype(np.float32),
        "xb": (n((N, T))).astype(np.float32),
        "ra": (np.random.uniform(0.5, 1.5, (1, T)) * ft).astype(np.float32),
        "rb": (np.random.uniform(0.5, 1.5, (1, T)) / ft).astype(np.float32),
        "sa_words": sap[0],
        "sa_scales": sap[1],
        "sb_words": sbp[0],
        "sb_scales": sbp[1],
    }


def reference(xa, xb, ra, rb, sa_words, sa_scales, sb_words, sb_scales):
    sau = unpack_weight(sa_words, sa_scales, "e2m1")
    sbu = unpack_weight(sb_words, sb_scales, "e4m3")
    da = f64(xa) * f64(ra)
    bl = np.pad(f64(xb), ((0, 0), (1, 0)))[:, :T]
    db = bl * f64(rb)
    ta = da.T
    tb = db.T
    taq = mxq(ta, 0, "e4m3")
    tbq = mxq(tb, 0, "e5m2")
    v = taq.T @ tbq + sau.T @ sbu
    y = 0.03 * v
    words, scales = planes(y)
    return y, words, scales

@@ -1,0 +1,281 @@
+from contextlib import ExitStack
+
+import concourse.mybir as mybir
+from concourse.masks import make_identity
+
+K, N, T, S = 512, 512, 1024, 1024
+FLOPS = 2 * K * N * (T + S)
+
+F32 = mybir.dt.float32
+BF16 = mybir.dt.bfloat16
+I32 = mybir.dt.int32
+U32 = mybir.dt.uint32
+U8 = mybir.dt.uint8
+E4M3 = mybir.dt.float8_e4m3fn_x4
+E5M2 = mybir.dt.float8_e5m2_x4
+E2M1 = mybir.dt.float4_e2m1fn_x4
+MULT = mybir.AluOpType.mult
+COPY = mybir.ActivationFunctionType.Copy
+
+P = 128
+PACK = 4
+PASS = P * PACK
+PASSES = T // PASS
+TILES = K // P
+RUN = 16
+PAD = 8
+OUT_SCALE = 0.03
+HALF = N // 2
+SPLIT = 384
+
+
+def tile_mix_lagged_moments_pl_kernel(tc, xa, xb, ra, rb, sa_words, sa_scales, sb_words, sb_scales, out_0, out_1, out_2):
+    nc = tc.nc
+    with ExitStack() as ctx:
+        keep = ctx.enter_context(tc.tile_pool(name="keep", bufs=1))
+        work = ctx.enter_context(tc.tile_pool(name="work", bufs=3))
+        psum = ctx.enter_context(tc.psum_pool(name="psum", bufs=1))
+        ctx.enter_context(tc.manual_schedule())
+
+        sa_scale_raw = keep.tile([P, PASSES, K], U8, align_bytes=64)
+        sb_scale = keep.tile([P, PASSES, N], U8, align_bytes=64)
+        nc.vector.memset(sa_scale_raw[:].rearrange("p z c -> p (z c)").bitcast(I32), 0)
+        nc.vector.memset(sb_scale[:].rearrange("p z c -> p (z c)").bitcast(I32), 0)
+
+        ident = keep.tile([P, P], F32)
+        make_identity(nc, ident[:])
+
+        xb_sb = [keep.tile([P, PAD + T], F32, name="xb_sb%d" % b) for b in range(TILES)]
+        for b in range(TILES):
+            nc.gpsimd.memset(xb_sb[b][:, PAD - 1 : PAD], 0.0)
+
+        def load_weights(r, name):
+            col = keep.tile([P, PASSES, PACK], F32, name=name)
+            nc.sync.dma_start(out=col[:], in_=r.rearrange("o (z n m) -> n (o z) m", z=PASSES, m=PACK))
+            return col
+
+        def load_scales(plane, scales):
+            for q in range(4):
+                nc.sync.dma_start(
+                    out=plane[32 * q : 32 * q + 4, :, :].bitcast(I32),
+                    in_=scales[:, 4 * q : 4 * q + 4, :].rearrange("z r c -> r z c").bitcast(I32),
+                )
+
+        def load_xb(b):
+            nc.sync.dma_start(out=xb_sb[b][:, PAD:], in_=xb[P * b : P * (b + 1), :])
+
+        xa_rows = xa.rearrange("(p j) t -> j p t", j=PACK)
+        out_rows = out_0.rearrange("(p j) n -> j p n", j=PACK)
+
+        rb_col = load_weights(rb, "rb_col")
+        sa_raw = keep.tile([P, PASSES, 2 * K], U8, align_bytes=64)
+        nc.sync.dma_start(out=sa_raw[:].bitcast(I32), in_=sa_words.rearrange("z p c -> p z c").bitcast(I32))
+        load_scales(sa_scale_raw, sa_scales)
+        load_xb(0)
+        ra_col = load_weights(ra, "ra_col")
+        load_xb(1)
+        sb_codes = keep.tile([P, PASSES, N], U32, align_bytes=64)
+        nc.sync.dma_start(out=sb_codes[:].bitcast(I32), in_=sb_words.rearrange("z p c r -> p z (c r)").bitcast(I32))
+        load_scales(sb_scale, sb_scales)
+        load_xb(2)
+        load_xb(3)
+        xa_src = []
+        for j in range(TILES - 1):
+            xa_sb = keep.tile([P, T], F32, name="xa_sb%d" % j)
+            nc.sync.dma_start(out=xa_sb[:], in_=xa_rows[j])
+            xa_src.append([xa_sb[:, PASS * z : PASS * (z + 1)] for z in range(PASSES)])
+        last = []
+        for z in range(PASSES):
+            xa_half = keep.tile([P, PASS], F32, name="xa_half%d" % z)
+            nc.sync.dma_start(out=xa_half[:], in_=xa_rows[TILES - 1][:, PASS * z : PASS * (z + 1)])
+            last.append(xa_half[:])
+        xa_src.append(last)
+        xb_src = [[xb_sb[b][:, PAD - 1 + PASS * z : PAD - 1 + PASS * (z + 1)] for z in range(PASSES)] for b in range(TILES)]
+
+        def halves(ap):
+            return ap.rearrange("p (g u i) -> p u g i", u=2, i=RUN)
+
+        def spread(col, tags, name):
+            banks = []
+            for z in range(PASSES):
+                bank = psum.tile([P, PASS], F32, tag=tags[z], name="%s_bank%d" % (name, z))
+                for m in range(PACK):
+                    nc.tensor.transpose(bank[:, m::PACK], col[:, z, m : m + 1].to_broadcast([P, P]), ident[:])
+                banks.append(bank)
+            part = keep.tile([P, PASS // 2], F32, name=name + "_part")
+            nc.scalar.activation(out=part[:].rearrange("p (g i) -> p g i", i=RUN), in_=halves(banks[1][:])[:, 1], func=COPY)
+            return banks, part
+
+        rb_banks, rb_part = spread(rb_col, ("late0", "late1"), "rb")
+        ra_banks, ra_part = spread(ra_col, ("ra0", "ra1"), "ra")
+
+        sa_codes = keep.tile([P, PASSES, TILES, 2 * P], U8, align_bytes=64)
+        nc.vector.tensor_copy(
+            out=sa_codes[:].rearrange("p z j (c b) -> p z j c b", b=2),
+            in_=sa_raw[:].rearrange("p z (c j b) -> p z j c b", j=PACK, b=2),
+        )
+        sa_scale = keep.tile([P, PASSES, TILES, P], U8, align_bytes=64)
+        nc.vector.tensor_copy(out=sa_scale[:], in_=sa_scale_raw[:].rearrange("p z (c j) -> p z j c", j=PACK))
+
+        tb_codes = [keep.tile([P, N], U32, align_bytes=64, name="tb_codes%d" % z) for z in range(PASSES)]
+        tb_scale = [keep.tile([P, N], U8, align_bytes=64, name="tb_scale%d" % z) for z in range(PASSES)]
+        ta_codes = [keep.tile([P, PASSES, P], U32, align_bytes=64, name="ta_codes%d" % j) for j in range(TILES)]
+        ta_scale = [keep.tile([P, PASSES, P], U8, align_bytes=64, name="ta_scale%d" % j) for j in range(TILES)]
+        y = keep.tile([P, TILES, N], F32, align_bytes=64)
+        acc = {}
+
+        def weigh(src, banks, part, zs):
+            words = []
+            if 0 in zs:
+                first = work.tile([P, PASS], BF16, align_bytes=64)
+                nc.vector.tensor_tensor(
+                    out=first[:].rearrange("p (u g i) -> p g u i", u=2, i=RUN),
+                    in0=src[0].rearrange("p (g u i) -> p g u i", u=2, i=RUN),
+                    in1=banks[0][:].rearrange("p (g u i) -> p g u i", u=2, i=RUN),
+                    op=MULT,
+                )
+                words.extend([first[:].bitcast(F32)[:, :P], first[:].bitcast(F32)[:, P:]])
+            if 1 in zs:
+                upper = work.tile([P, PASS // 2], BF16, align_bytes=64)
+                nc.gpsimd.tensor_tensor(
+                    out=upper[:].rearrange("p (g i) -> p g i", i=RUN),
+                    in0=halves(src[1])[:, 1],
+                    in1=part[:].rearrange("p (g i) -> p g i", i=RUN),
+                    op=MULT,
+                )
+                lower = work.tile([P, PASS // 2], BF16, align_bytes=64)
+                nc.vector.tensor_tensor(
+                    out=lower[:].rearrange("p (g i) -> p g i", i=RUN),
+                    in0=halves(src[1])[:, 0],
+                    in1=halves(banks[1][:])[:, 0],
+                    op=MULT,
+                )
+                words.extend([lower[:].bitcast(F32), upper[:].bitcast(F32)])
+            return words
+
+        def turn(words):
+            count = len(words) // 2
+            bank = psum.tile([P, PASSES, 2, P], F32, tag="turn", bufs=2)
+            for w, src in enumerate(words):
+                nc.tensor.transpose(bank[:, w // 2, w % 2, :], src, ident[:])
+            grouped = work.tile([P, PASSES, P, PACK], BF16, align_bytes=64)
+            nc.scalar.copy(
+                out=grouped[:, :count].bitcast(F32),
+                in_=bank[:, :count].rearrange("p z u c -> p z c u"),
+            )
+            return grouped
+
+        def quantise_b(b, grouped):
+            cols = slice(P * b, P * (b + 1))
+            for z in range(PASSES):
+                nc.vector.quantize_mx(
+                    out=tb_codes[z][:, cols].bitcast(E5M2),
+                    scales=tb_scale[z][:, cols],
+                    in_=grouped[:, z].rearrange("p c r -> p (c r)"),
+                )
+
+        def quantise_a(j, grouped, z0, count):
+            nc.vector.quantize_mx(
+                out=ta_codes[j][:, z0 : z0 + count].rearrange("p z c -> p (z c)").bitcast(E4M3),
+                scales=ta_scale[j][:, z0 : z0 + count].rearrange("p z c -> p (z c)"),
+                in_=grouped[:, :count].rearrange("p z c r -> p (z c r)"),
+            )
+
+        def stored_product(j, tag):
+            acc[j] = psum.tile([P, N], F32, tag=tag, name="acc%d" % j)
+            for z in range(PASSES):
+                nc.tensor.matmul_mx(
+                    out=acc[j][:],
+                    lhsT=sa_codes[:, z, j, :].bitcast(E2M1),
+                    lhsT_scale=sa_scale[:, z, j, :],
+                    rhs=sb_codes[:, z, :].bitcast(E4M3),
+                    rhs_scale=sb_scale[:, z, :],
+                    start=(z == 0),
+                    stop=False,
+                )
+
+        def live_product(j, z):
+            nc.tensor.matmul_mx(
+                out=acc[j][:],
+                lhsT=ta_codes[j][:, z, :].bitcast(E4M3),
+                lhsT_scale=ta_scale[j][:, z, :],
+                rhs=tb_codes[z][:].bitcast(E5M2),
+                rhs_scale=tb_scale[z][:],
+                start=False,
+                stop=(z == PASSES - 1),
+            )
+
+        def scale_out(j, cols):
+            nc.scalar.activation(out=y[:, j, cols], in_=acc[j][:, cols], func=COPY, scale=OUT_SCALE)
+
+        def finish(j):
+            for z in range(PASSES):
+                live_product(j, z)
+            scale_out(j, slice(0, N))
+            nc.sync.dma_start(out=out_rows[j], in_=y[:, j, :])
+
+        both = (0, 1)
+        before = None
+        for b in range(TILES):
+            words = weigh(xb_src[b], rb_banks, rb_part, both)
+            if b > 0:
+                quantise_b(b - 1, before)
+            if b == 2:
+                stored_product(0, "acc0")
+                stored_product(1, "acc1")
+            before = turn(words)
+        for j in range(TILES - 1):
+            words = weigh(xa_src[j], ra_banks, ra_part, both)
+            if j == 0:
+                quantise_b(TILES - 1, before)
+                stored_product(2, "late0")
+                stored_product(3, "late1")
+                before = turn(words)
+            else:
+                quantise_a(j - 1, before, 0, PASSES)
+                before = turn(words)
+                finish(j - 1)
+        j = TILES - 1
+        grouped0 = turn(weigh(xa_src[j], ra_banks, ra_part, (0,)))
+        grouped1 = turn(weigh(xa_src[j], ra_banks, ra_part, (1,)))
+        quantise_a(j - 1, before, 0, PASSES)
+        finish(j - 1)
+        quantise_a(j, grouped0, 0, 1)
+        quantise_a(j, grouped1, 1, 1)
+        live_product(j, 0)
+        live_product(j, 1)
+
+        y_grouped = keep.tile([P, N, PACK], BF16, align_bytes=64)
+        y_codes = keep.tile([P, N], U32, align_bytes=64)
+        y_scale = keep.tile([P, N], U8, align_bytes=64)
+
+        def interleave(copy, c0, c1):
+            copy(
+                out=y_grouped[:, c0:c1, :].rearrange("p (c i) j -> p c j i", i=4),
+                in_=y[:, :, c0:c1].rearrange("p j (c i) -> p c j i", i=4),
+            )
+
+        def quantise_y(c0, c1):
+            nc.vector.quantize_mx(
+                out=y_codes[:, c0:c1].bitcast(E4M3),
+                scales=y_scale[:, c0:c1],
+                in_=y_grouped[:, c0:c1, :].rearrange("p c j -> p (c j)"),
+            )
+
+        scale_out(j, slice(0, HALF))
+        scale_out(j, slice(HALF, N))
+        nc.sync.dma_start(out=out_rows[j], in_=y[:, j, :])
+        interleave(nc.vector.tensor_copy, 0, HALF)
+        interleave(nc.scalar.copy, SPLIT, N)
+        interleave(nc.vector.tensor_copy, HALF, SPLIT)
+        words_out = out_1.rearrange("z p c r -> p (z c r)").bitcast(I32)
+        quantise_y(0, HALF)
+        nc.sync.dma_start(out=words_out[:, :HALF], in_=y_codes[:, :HALF].bitcast(I32))
+        quantise_y(HALF, N)
+        nc.sync.dma_start(out=words_out[:, HALF:], in_=y_codes[:, HALF:].bitcast(I32))
+        for q in range(4):
+            queue = nc.scalar if q % 2 == 0 else nc.sync
+            queue.dma_start(
+                out=out_2[0, 4 * q : 4 * q + 4, :].bitcast(I32),
+                in_=y_scale[32 * q : 32 * q + 4, :].bitcast(I32),
+            )

@@ -46,8 +46,10 @@ def tile_mix_lagged_moments_pl_kernel(tc, xa, xb, ra, rb, sa_words, sa_scales, s
         make_identity(nc, ident[:])
 
         xb_sb = [keep.tile([P, PAD + T], F32, name="xb_sb%d" % b) for b in range(TILES)]
+        zero = keep.tile([P, 1], F32)
+        nc.vector.memset(zero[:], 0.0)
         for b in range(TILES):
-            nc.gpsimd.memset(xb_sb[b][:, PAD - 1 : PAD], 0.0)
+            nc.scalar.activation(out=xb_sb[b][:, PAD - 1 : PAD], in_=zero[:], func=COPY)
 
         def load_weights(r, name):
             col = keep.tile([P, PASSES, PACK], F32, name=name)
@@ -67,18 +69,18 @@ def tile_mix_lagged_moments_pl_kernel(tc, xa, xb, ra, rb, sa_words, sa_scales, s
         xa_rows = xa.rearrange("(p j) t -> j p t", j=PACK)
         out_rows = out_0.rearrange("(p j) n -> j p n", j=PACK)
 
-        rb_col = load_weights(rb, "rb_col")
         sa_raw = keep.tile([P, PASSES, 2 * K], U8, align_bytes=64)
         nc.sync.dma_start(out=sa_raw[:].bitcast(I32), in_=sa_words.rearrange("z p c -> p z c").bitcast(I32))
+        rb_col = load_weights(rb, "rb_col")
         load_scales(sa_scale_raw, sa_scales)
         load_xb(0)
-        ra_col = load_weights(ra, "ra_col")
         load_xb(1)
-        sb_codes = keep.tile([P, PASSES, N], U32, align_bytes=64)
-        nc.sync.dma_start(out=sb_codes[:].bitcast(I32), in_=sb_words.rearrange("z p c r -> p z (c r)").bitcast(I32))
-        load_scales(sb_scale, sb_scales)
+        ra_col = load_weights(ra, "ra_col")
         load_xb(2)
         load_xb(3)
+        sb_codes = keep.tile([P, PASSES, N], U32, align_bytes=64)
+        load_scales(sb_scale, sb_scales)
+        nc.sync.dma_start(out=sb_codes[:].bitcast(I32), in_=sb_words.rearrange("z p c r -> p z (c r)").bitcast(I32))
         xa_src = []
         for j in range(TILES - 1):
             xa_sb = keep.tile([P, T], F32, name="xa_sb%d" % j)
@@ -92,22 +94,16 @@ def tile_mix_lagged_moments_pl_kernel(tc, xa, xb, ra, rb, sa_words, sa_scales, s
         xa_src.append(last)
         xb_src = [[xb_sb[b][:, PAD - 1 + PASS * z : PAD - 1 + PASS * (z + 1)] for z in range(PASSES)] for b in range(TILES)]
 
-        def halves(ap):
-            return ap.rearrange("p (g u i) -> p u g i", u=2, i=RUN)
-
         def spread(col, tags, name):
             banks = []
             for z in range(PASSES):
-                bank = psum.tile([P, PASS], F32, tag=tags[z], name="%s_bank%d" % (name, z))
+                bank = psum.tile([P, PACK, P], F32, tag=tags[z], name="%s_bank%d" % (name, z))
                 for m in range(PACK):
-                    nc.tensor.transpose(bank[:, m::PACK], col[:, z, m : m + 1].to_broadcast([P, P]), ident[:])
+                    nc.tensor.transpose(bank[:, m, :], col[:, z, m : m + 1].to_broadcast([P, P]), ident[:])
                 banks.append(bank)
-            part = keep.tile([P, PASS // 2], F32, name=name + "_part")
-            nc.scalar.activation(out=part[:].rearrange("p (g i) -> p g i", i=RUN), in_=halves(banks[1][:])[:, 1], func=COPY)
-            return banks, part
+            return banks
 
-        rb_banks, rb_part = spread(rb_col, ("late0", "late1"), "rb")
-        ra_banks, ra_part = spread(ra_col, ("ra0", "ra1"), "ra")
+        rb_banks = spread(rb_col, ("late0", "late1"), "rb")
 
         sa_codes = keep.tile([P, PASSES, TILES, 2 * P], U8, align_bytes=64)
         nc.vector.tensor_copy(
@@ -124,33 +120,17 @@ def tile_mix_lagged_moments_pl_kernel(tc, xa, xb, ra, rb, sa_words, sa_scales, s
         y = keep.tile([P, TILES, N], F32, align_bytes=64)
         acc = {}
 
-        def weigh(src, banks, part, zs):
+        def weigh(src, banks, zs):
             words = []
-            if 0 in zs:
-                first = work.tile([P, PASS], BF16, align_bytes=64)
+            for z in zs:
+                prod = work.tile([P, PASS], BF16, align_bytes=64, bufs=4)
                 nc.vector.tensor_tensor(
-                    out=first[:].rearrange("p (u g i) -> p g u i", u=2, i=RUN),
-                    in0=src[0].rearrange("p (g u i) -> p g u i", u=2, i=RUN),
-                    in1=banks[0][:].rearrange("p (g u i) -> p g u i", u=2, i=RUN),
+                    out=prod[:].rearrange("p (u g a m) -> p g u a m", u=2, a=RUN // PACK, m=PACK),
+                    in0=src[z].rearrange("p (g u a m) -> p g u a m", u=2, a=RUN // PACK, m=PACK),
+                    in1=banks[z][:].rearrange("p m (g u a) -> p g u a m", u=2, a=RUN // PACK),
                     op=MULT,
                 )
-                words.extend([first[:].bitcast(F32)[:, :P], first[:].bitcast(F32)[:, P:]])
-            if 1 in zs:
-                upper = work.tile([P, PASS // 2], BF16, align_bytes=64)
-                nc.gpsimd.tensor_tensor(
-                    out=upper[:].rearrange("p (g i) -> p g i", i=RUN),
-                    in0=halves(src[1])[:, 1],
-                    in1=part[:].rearrange("p (g i) -> p g i", i=RUN),
-                    op=MULT,
-                )
-                lower = work.tile([P, PASS // 2], BF16, align_bytes=64)
-                nc.vector.tensor_tensor(
-                    out=lower[:].rearrange("p (g i) -> p g i", i=RUN),
-                    in0=halves(src[1])[:, 0],
-                    in1=halves(banks[1][:])[:, 0],
-                    op=MULT,
-                )
-                words.extend([lower[:].bitcast(F32), upper[:].bitcast(F32)])
+                words.extend([prod[:].bitcast(F32)[:, :P], prod[:].bitcast(F32)[:, P:]])
             return words
 
         def turn(words):
@@ -216,28 +196,28 @@ def tile_mix_lagged_moments_pl_kernel(tc, xa, xb, ra, rb, sa_words, sa_scales, s
 
         both = (0, 1)
         before = None
+        ra_banks = None
         for b in range(TILES):
-            words = weigh(xb_src[b], rb_banks, rb_part, both)
+            words = weigh(xb_src[b], rb_banks, both)
             if b > 0:
                 quantise_b(b - 1, before)
-            if b == 2:
-                stored_product(0, "acc0")
-                stored_product(1, "acc1")
             before = turn(words)
+            if b == 0:
+                ra_banks = spread(ra_col, ("ra0", "ra1"), "ra")
+        stored_product(0, "acc0")
         for j in range(TILES - 1):
-            words = weigh(xa_src[j], ra_banks, ra_part, both)
+            words = weigh(xa_src[j], ra_banks, both)
             if j == 0:
                 quantise_b(TILES - 1, before)
-                stored_product(2, "late0")
-                stored_product(3, "late1")
                 before = turn(words)
             else:
                 quantise_a(j - 1, before, 0, PASSES)
                 before = turn(words)
                 finish(j - 1)
+            stored_product(j + 1, ("acc1", "late0", "late1")[j])
         j = TILES - 1
-        grouped0 = turn(weigh(xa_src[j], ra_banks, ra_part, (0,)))
-        grouped1 = turn(weigh(xa_src[j], ra_banks, ra_part, (1,)))
+        grouped0 = turn(weigh(xa_src[j], ra_banks, (0,)))
+        grouped1 = turn(weigh(xa_src[j], ra_banks, (1,)))
         quantise_a(j - 1, before, 0, PASSES)
         finish(j - 1)
         quantise_a(j, grouped0, 0, 1)

@@ -26,7 +26,9 @@ RUN = 16
 PAD = 8
 OUT_SCALE = 0.03
 HALF = N // 2
-SPLIT = 384
+ROWS = T // P
+STEPS = 2 * TILES * PASSES
+LAG = 3
 
 
 def tile_mix_lagged_moments_pl_kernel(tc, xa, xb, ra, rb, sa_words, sa_scales, sb_words, sb_scales, out_0, out_1, out_2):
@@ -37,24 +39,19 @@ def tile_mix_lagged_moments_pl_kernel(tc, xa, xb, ra, rb, sa_words, sa_scales, s
         psum = ctx.enter_context(tc.psum_pool(name="psum", bufs=1))
         ctx.enter_context(tc.manual_schedule())
 
+        rows = keep.tile([P, P + PAD], F32)
+        nc.gpsimd.memset(rows[:], 0.0)
+        ident = keep.tile([P, P], F32)
+        make_identity(nc, ident[:])
+
         sa_scale_raw = keep.tile([P, PASSES, K], U8, align_bytes=64)
         sb_scale = keep.tile([P, PASSES, N], U8, align_bytes=64)
         nc.vector.memset(sa_scale_raw[:].rearrange("p z c -> p (z c)").bitcast(I32), 0)
         nc.vector.memset(sb_scale[:].rearrange("p z c -> p (z c)").bitcast(I32), 0)
 
-        ident = keep.tile([P, P], F32)
-        make_identity(nc, ident[:])
-
         xb_sb = [keep.tile([P, PAD + T], F32, name="xb_sb%d" % b) for b in range(TILES)]
-        zero = keep.tile([P, 1], F32)
-        nc.vector.memset(zero[:], 0.0)
         for b in range(TILES):
-            nc.scalar.activation(out=xb_sb[b][:, PAD - 1 : PAD], in_=zero[:], func=COPY)
-
-        def load_weights(r, name):
-            col = keep.tile([P, PASSES, PACK], F32, name=name)
-            nc.sync.dma_start(out=col[:], in_=r.rearrange("o (z n m) -> n (o z) m", z=PASSES, m=PACK))
-            return col
+            nc.scalar.activation(out=xb_sb[b][:, PAD - 1 : PAD], in_=rows[:, P : P + 1], func=COPY)
 
         def load_scales(plane, scales):
             for q in range(4):
@@ -63,47 +60,42 @@ def tile_mix_lagged_moments_pl_kernel(tc, xa, xb, ra, rb, sa_words, sa_scales, s
                     in_=scales[:, 4 * q : 4 * q + 4, :].rearrange("z r c -> r z c").bitcast(I32),
                 )
 
-        def load_xb(b):
-            nc.sync.dma_start(out=xb_sb[b][:, PAD:], in_=xb[P * b : P * (b + 1), :])
-
         xa_rows = xa.rearrange("(p j) t -> j p t", j=PACK)
         out_rows = out_0.rearrange("(p j) n -> j p n", j=PACK)
 
         sa_raw = keep.tile([P, PASSES, 2 * K], U8, align_bytes=64)
         nc.sync.dma_start(out=sa_raw[:].bitcast(I32), in_=sa_words.rearrange("z p c -> p z c").bitcast(I32))
-        rb_col = load_weights(rb, "rb_col")
+        nc.sync.dma_start(out=rows[0:ROWS, :P], in_=rb.rearrange("o (m n) -> (o m) n", n=P))
+        nc.sync.dma_start(out=rows[ROWS : 2 * ROWS, :P], in_=ra.rearrange("o (m n) -> (o m) n", n=P))
         load_scales(sa_scale_raw, sa_scales)
-        load_xb(0)
-        load_xb(1)
-        ra_col = load_weights(ra, "ra_col")
-        load_xb(2)
-        load_xb(3)
-        sb_codes = keep.tile([P, PASSES, N], U32, align_bytes=64)
+        for b in range(TILES):
+            nc.sync.dma_start(out=xb_sb[b][:, PAD:], in_=xb[P * b : P * (b + 1), :])
         load_scales(sb_scale, sb_scales)
+        sb_codes = keep.tile([P, PASSES, N], U32, align_bytes=64)
         nc.sync.dma_start(out=sb_codes[:].bitcast(I32), in_=sb_words.rearrange("z p c r -> p z (c r)").bitcast(I32))
-        xa_src = []
+        xa_sb = [keep.tile([P, T], F32, name="xa_sb%d" % j) for j in range(TILES - 1)]
         for j in range(TILES - 1):
-            xa_sb = keep.tile([P, T], F32, name="xa_sb%d" % j)
-            nc.sync.dma_start(out=xa_sb[:], in_=xa_rows[j])
-            xa_src.append([xa_sb[:, PASS * z : PASS * (z + 1)] for z in range(PASSES)])
-        last = []
+            nc.sync.dma_start(out=xa_sb[j][:], in_=xa_rows[j])
+        xa_last = [keep.tile([P, PASS], F32, name="xa_last%d" % z) for z in range(PASSES)]
         for z in range(PASSES):
-            xa_half = keep.tile([P, PASS], F32, name="xa_half%d" % z)
-            nc.sync.dma_start(out=xa_half[:], in_=xa_rows[TILES - 1][:, PASS * z : PASS * (z + 1)])
-            last.append(xa_half[:])
-        xa_src.append(last)
-        xb_src = [[xb_sb[b][:, PAD - 1 + PASS * z : PAD - 1 + PASS * (z + 1)] for z in range(PASSES)] for b in range(TILES)]
+            nc.sync.dma_start(out=xa_last[z][:], in_=xa_rows[TILES - 1][:, PASS * z : PASS * (z + 1)])
 
-        def spread(col, tags, name):
-            banks = []
-            for z in range(PASSES):
-                bank = psum.tile([P, PACK, P], F32, tag=tags[z], name="%s_bank%d" % (name, z))
-                for m in range(PACK):
-                    nc.tensor.transpose(bank[:, m, :], col[:, z, m : m + 1].to_broadcast([P, P]), ident[:])
-                banks.append(bank)
-            return banks
+        rows_turned = psum.tile([P, P], F32, tag="acc2")
+        nc.tensor.transpose(rows_turned[:], rows[:, :P], ident[:])
+        cols = keep.tile([P, 2 * ROWS], F32)
+        nc.scalar.copy(out=cols[:], in_=rows_turned[:, : 2 * ROWS])
 
-        rb_banks = spread(rb_col, ("late0", "late1"), "rb")
+        def spread(first, tag):
+            bank = psum.tile([P, PASS], F32, tag=tag)
+            for m in range(PACK):
+                nc.tensor.transpose(bank[:, P * m : P * (m + 1)], cols[:, first + m : first + m + 1].to_broadcast([P, P]), ident[:])
+            return bank
+
+        rb_banks = [spread(PACK * z, "spare%d" % z) for z in range(PASSES)]
+        ra_row = keep.tile([P, PASSES, PASS], F32)
+
+        def spread_ra(z):
+            nc.scalar.copy(out=ra_row[:, z, :], in_=spread(ROWS + PACK * z, "acc%d" % (2 + z))[:])
 
         sa_codes = keep.tile([P, PASSES, TILES, 2 * P], U8, align_bytes=64)
         nc.vector.tensor_copy(
@@ -120,49 +112,59 @@ def tile_mix_lagged_moments_pl_kernel(tc, xa, xb, ra, rb, sa_words, sa_scales, s
         y = keep.tile([P, TILES, N], F32, align_bytes=64)
         acc = {}
 
-        def weigh(src, banks, zs):
-            words = []
-            for z in zs:
-                prod = work.tile([P, PASS], BF16, align_bytes=64, bufs=4)
-                nc.vector.tensor_tensor(
-                    out=prod[:].rearrange("p (u g a m) -> p g u a m", u=2, a=RUN // PACK, m=PACK),
-                    in0=src[z].rearrange("p (g u a m) -> p g u a m", u=2, a=RUN // PACK, m=PACK),
-                    in1=banks[z][:].rearrange("p m (g u a) -> p g u a m", u=2, a=RUN // PACK),
-                    op=MULT,
-                )
-                words.extend([prod[:].bitcast(F32)[:, :P], prod[:].bitcast(F32)[:, P:]])
-            return words
+        tb_grouped = [keep.tile([P, 2 * P, PACK], BF16, align_bytes=64, name="tb_grouped%d" % i) for i in range(2 * PASSES)]
+        ta_grouped = {}
 
-        def turn(words):
-            count = len(words) // 2
-            bank = psum.tile([P, PASSES, 2, P], F32, tag="turn", bufs=2)
-            for w, src in enumerate(words):
-                nc.tensor.transpose(bank[:, w // 2, w % 2, :], src, ident[:])
-            grouped = work.tile([P, PASSES, P, PACK], BF16, align_bytes=64)
-            nc.scalar.copy(
-                out=grouped[:, :count].bitcast(F32),
-                in_=bank[:, :count].rearrange("p z u c -> p z c u"),
+        def weigh(step):
+            tile, z = divmod(step, PASSES)
+            if tile < TILES:
+                src = xb_sb[tile][:, PAD - 1 + PASS * z : PAD - 1 + PASS * (z + 1)]
+                weights = rb_banks[z][:]
+            else:
+                j = tile - TILES
+                src = xa_sb[j][:, PASS * z : PASS * (z + 1)] if j < TILES - 1 else xa_last[z][:]
+                weights = ra_row[:, z, :]
+            prod = work.tile([P, PASS], BF16, align_bytes=64, bufs=6)
+            nc.vector.tensor_tensor(
+                out=prod[:].rearrange("p (u g i) -> p g u i", u=2, i=RUN),
+                in0=src.rearrange("p (g u i) -> p g u i", u=2, i=RUN),
+                in1=weights.rearrange("p (g u i) -> p g u i", u=2, i=RUN),
+                op=MULT,
             )
-            return grouped
+            return prod
 
-        def quantise_b(b, grouped):
-            cols = slice(P * b, P * (b + 1))
-            for z in range(PASSES):
+        def turn(step, prod):
+            tile, z = divmod(step, PASSES)
+            tags = ("turn0", "turn1") if tile < TILES else ("spare0", "spare1", "turn0", "turn1")
+            bank = psum.tile([P, 2, P], F32, tag=tags[step % len(tags)])
+            for u in range(2):
+                nc.tensor.transpose(bank[:, u, :], prod[:].bitcast(F32)[:, P * u : P * (u + 1)], ident[:])
+            if tile < TILES:
+                grouped = tb_grouped[PASSES * (tile // 2) + z][:, P * (tile % 2) : P * (tile % 2 + 1), :]
+            else:
+                ta_tile = work.tile([P, P, PACK], BF16, align_bytes=64, bufs=LAG + 2)
+                ta_grouped[step] = ta_tile
+                grouped = ta_tile[:]
+            nc.scalar.copy(out=grouped.bitcast(F32), in_=bank[:].rearrange("p u c -> p c u"))
+
+        def quantise(step):
+            tile, z = divmod(step, PASSES)
+            if tile >= TILES:
                 nc.vector.quantize_mx(
-                    out=tb_codes[z][:, cols].bitcast(E5M2),
-                    scales=tb_scale[z][:, cols],
-                    in_=grouped[:, z].rearrange("p c r -> p (c r)"),
+                    out=ta_codes[tile - TILES][:, z, :].bitcast(E4M3),
+                    scales=ta_scale[tile - TILES][:, z, :],
+                    in_=ta_grouped[step][:].rearrange("p c r -> p (c r)"),
+                )
+            elif tile % 2 == 1:
+                half = slice(HALF * (tile // 2), HALF * (tile // 2 + 1))
+                nc.vector.quantize_mx(
+                    out=tb_codes[z][:, half].bitcast(E5M2),
+                    scales=tb_scale[z][:, half],
+                    in_=tb_grouped[PASSES * (tile // 2) + z][:].rearrange("p c r -> p (c r)"),
                 )
 
-        def quantise_a(j, grouped, z0, count):
-            nc.vector.quantize_mx(
-                out=ta_codes[j][:, z0 : z0 + count].rearrange("p z c -> p (z c)").bitcast(E4M3),
-                scales=ta_scale[j][:, z0 : z0 + count].rearrange("p z c -> p (z c)"),
-                in_=grouped[:, :count].rearrange("p z c r -> p (z c r)"),
-            )
-
-        def stored_product(j, tag):
-            acc[j] = psum.tile([P, N], F32, tag=tag, name="acc%d" % j)
+        def stored_product(j):
+            acc[j] = psum.tile([P, N], F32, tag="acc%d" % j, name="acc%d" % j)
             for z in range(PASSES):
                 nc.tensor.matmul_mx(
                     out=acc[j][:],
@@ -188,42 +190,35 @@ def tile_mix_lagged_moments_pl_kernel(tc, xa, xb, ra, rb, sa_words, sa_scales, s
         def scale_out(j, cols):
             nc.scalar.activation(out=y[:, j, cols], in_=acc[j][:, cols], func=COPY, scale=OUT_SCALE)
 
-        def finish(j):
-            for z in range(PASSES):
-                live_product(j, z)
+        def store(j):
             scale_out(j, slice(0, N))
             nc.sync.dma_start(out=out_rows[j], in_=y[:, j, :])
 
-        both = (0, 1)
-        before = None
-        ra_banks = None
-        for b in range(TILES):
-            words = weigh(xb_src[b], rb_banks, both)
-            if b > 0:
-                quantise_b(b - 1, before)
-            before = turn(words)
-            if b == 0:
-                ra_banks = spread(ra_col, ("ra0", "ra1"), "ra")
-        stored_product(0, "acc0")
-        for j in range(TILES - 1):
-            words = weigh(xa_src[j], ra_banks, both)
-            if j == 0:
-                quantise_b(TILES - 1, before)
-                before = turn(words)
-            else:
-                quantise_a(j - 1, before, 0, PASSES)
-                before = turn(words)
-                finish(j - 1)
-            stored_product(j + 1, ("acc1", "late0", "late1")[j])
+        def multiply(step):
+            tile, z = divmod(step, PASSES)
+            if tile >= TILES:
+                live_product(tile - TILES, z)
+
+        for step in range(STEPS):
+            prod = weigh(step)
+            if step >= LAG:
+                quantise(step - LAG)
+            turn(step, prod)
+            done, z = divmod(step - LAG - 1 - STEPS // 2, PASSES)
+            if done >= 0 and z == PASSES - 1:
+                store(done)
+            if step in (2, 3):
+                spread_ra(step - 2)
+            if step >= 6 and step % 2 == 0 and step < 6 + 2 * TILES:
+                stored_product((step - 6) // 2)
+            if step >= LAG:
+                multiply(step - LAG)
         j = TILES - 1
-        grouped0 = turn(weigh(xa_src[j], ra_banks, (0,)))
-        grouped1 = turn(weigh(xa_src[j], ra_banks, (1,)))
-        quantise_a(j - 1, before, 0, PASSES)
-        finish(j - 1)
-        quantise_a(j, grouped0, 0, 1)
-        quantise_a(j, grouped1, 1, 1)
-        live_product(j, 0)
-        live_product(j, 1)
+        for step in range(STEPS - LAG, STEPS):
+            quantise(step)
+            multiply(step)
+        nc.vector.tensor_scalar(out=y[:, j - 1, :], in0=acc[j - 1][:], scalar1=OUT_SCALE, scalar2=None, op0=MULT)
+        nc.sync.dma_start(out=out_rows[j - 1], in_=y[:, j - 1, :])
 
         y_grouped = keep.tile([P, N, PACK], BF16, align_bytes=64)
         y_codes = keep.tile([P, N], U32, align_bytes=64)
@@ -242,12 +237,12 @@ def tile_mix_lagged_moments_pl_kernel(tc, xa, xb, ra, rb, sa_words, sa_scales, s
                 in_=y_grouped[:, c0:c1, :].rearrange("p c j -> p (c j)"),
             )
 
-        scale_out(j, slice(0, HALF))
-        scale_out(j, slice(HALF, N))
+        for c in range(0, N, P):
+            scale_out(j, slice(c, c + P))
         nc.sync.dma_start(out=out_rows[j], in_=y[:, j, :])
-        interleave(nc.vector.tensor_copy, 0, HALF)
-        interleave(nc.scalar.copy, SPLIT, N)
-        interleave(nc.vector.tensor_copy, HALF, SPLIT)
+        for c in range(0, N - P, P):
+            interleave(nc.vector.tensor_copy, c, c + P)
+        interleave(nc.scalar.copy, N - P, N)
         words_out = out_1.rearrange("z p c r -> p (z c r)").bitcast(I32)
         quantise_y(0, HALF)
         nc.sync.dma_start(out=words_out[:, :HALF], in_=y_codes[:, :HALF].bitcast(I32))

@@ -53,26 +53,33 @@ def tile_mix_lagged_moments_pl_kernel(tc, xa, xb, ra, rb, sa_words, sa_scales, s
         for b in range(TILES):
             nc.scalar.activation(out=xb_sb[b][:, PAD - 1 : PAD], in_=rows[:, P : P + 1], func=COPY)
 
-        def load_scales(plane, scales):
-            for q in range(4):
+        def load_scales(plane, scales, quadrants):
+            for q in quadrants:
                 nc.sync.dma_start(
                     out=plane[32 * q : 32 * q + 4, :, :].bitcast(I32),
                     in_=scales[:, 4 * q : 4 * q + 4, :].rearrange("z r c -> r z c").bitcast(I32),
                 )
 
         xa_rows = xa.rearrange("(p j) t -> j p t", j=PACK)
-        out_rows = out_0.rearrange("(p j) n -> j p n", j=PACK)
+        out_rows = out_0.rearrange("(p j) n -> p j n", j=PACK)
+
+        def load_xb(b):
+            nc.sync.dma_start(out=xb_sb[b][:, PAD:], in_=xb[P * b : P * (b + 1), :])
 
         sa_raw = keep.tile([P, PASSES, 2 * K], U8, align_bytes=64)
         nc.sync.dma_start(out=sa_raw[:].bitcast(I32), in_=sa_words.rearrange("z p c -> p z c").bitcast(I32))
         nc.sync.dma_start(out=rows[0:ROWS, :P], in_=rb.rearrange("o (m n) -> (o m) n", n=P))
         nc.sync.dma_start(out=rows[ROWS : 2 * ROWS, :P], in_=ra.rearrange("o (m n) -> (o m) n", n=P))
-        load_scales(sa_scale_raw, sa_scales)
-        for b in range(TILES):
-            nc.sync.dma_start(out=xb_sb[b][:, PAD:], in_=xb[P * b : P * (b + 1), :])
-        load_scales(sb_scale, sb_scales)
+        load_xb(0)
+        load_xb(1)
+        load_scales(sa_scale_raw, sa_scales, (0, 1))
+        load_xb(2)
+        load_scales(sa_scale_raw, sa_scales, (2, 3))
+        load_xb(3)
+        load_scales(sb_scale, sb_scales, (0, 1))
         sb_codes = keep.tile([P, PASSES, N], U32, align_bytes=64)
         nc.sync.dma_start(out=sb_codes[:].bitcast(I32), in_=sb_words.rearrange("z p c r -> p z (c r)").bitcast(I32))
+        load_scales(sb_scale, sb_scales, (2, 3))
         xa_sb = [keep.tile([P, T], F32, name="xa_sb%d" % j) for j in range(TILES - 1)]
         for j in range(TILES - 1):
             nc.sync.dma_start(out=xa_sb[j][:], in_=xa_rows[j])
@@ -103,7 +110,6 @@ def tile_mix_lagged_moments_pl_kernel(tc, xa, xb, ra, rb, sa_words, sa_scales, s
             in_=sa_raw[:].rearrange("p z (c j b) -> p z j c b", j=PACK, b=2),
         )
         sa_scale = keep.tile([P, PASSES, TILES, P], U8, align_bytes=64)
-        nc.vector.tensor_copy(out=sa_scale[:], in_=sa_scale_raw[:].rearrange("p z (c j) -> p z j c", j=PACK))
 
         tb_codes = [keep.tile([P, N], U32, align_bytes=64, name="tb_codes%d" % z) for z in range(PASSES)]
         tb_scale = [keep.tile([P, N], U8, align_bytes=64, name="tb_scale%d" % z) for z in range(PASSES)]
@@ -192,14 +198,12 @@ def tile_mix_lagged_moments_pl_kernel(tc, xa, xb, ra, rb, sa_words, sa_scales, s
 
         def store(j):
             scale_out(j, slice(0, N))
-            nc.sync.dma_start(out=out_rows[j], in_=y[:, j, :])
-
-        def multiply(step):
-            tile, z = divmod(step, PASSES)
-            if tile >= TILES:
-                live_product(tile - TILES, z)
+            if j == 0:
+                nc.sync.dma_start(out=out_rows[:, j, :], in_=y[:, j, :])
 
         for step in range(STEPS):
+            if step == 4:
+                nc.vector.tensor_copy(out=sa_scale[:], in_=sa_scale_raw[:].rearrange("p z (c j) -> p z j c", j=PACK))
             prod = weigh(step)
             if step >= LAG:
                 quantise(step - LAG)
@@ -209,16 +213,21 @@ def tile_mix_lagged_moments_pl_kernel(tc, xa, xb, ra, rb, sa_words, sa_scales, s
                 store(done)
             if step in (2, 3):
                 spread_ra(step - 2)
-            if step >= 6 and step % 2 == 0 and step < 6 + 2 * TILES:
-                stored_product((step - 6) // 2)
-            if step >= LAG:
-                multiply(step - LAG)
+            if step in range(5, 5 + 2 * TILES, 2):
+                stored_product((step - 5) // 2)
+            done, z = divmod(step - LAG - STEPS // 2, PASSES)
+            if done >= 0 and z == PASSES - 1:
+                live_product(done, 0)
+                live_product(done, 1)
         j = TILES - 1
-        for step in range(STEPS - LAG, STEPS):
-            quantise(step)
-            multiply(step)
+        quantise(STEPS - 3)
+        live_product(j - 1, 0)
+        live_product(j - 1, 1)
+        for z in range(PASSES):
+            quantise(STEPS - PASSES + z)
+            live_product(j, z)
         nc.vector.tensor_scalar(out=y[:, j - 1, :], in0=acc[j - 1][:], scalar1=OUT_SCALE, scalar2=None, op0=MULT)
-        nc.sync.dma_start(out=out_rows[j - 1], in_=y[:, j - 1, :])
+        nc.sync.dma_start(out=out_rows[:, 1:j, :], in_=y[:, 1:j, :])
 
         y_grouped = keep.tile([P, N, PACK], BF16, align_bytes=64)
         y_codes = keep.tile([P, N], U32, align_bytes=64)
@@ -239,7 +248,7 @@ def tile_mix_lagged_moments_pl_kernel(tc, xa, xb, ra, rb, sa_words, sa_scales, s
 
         for c in range(0, N, P):
             scale_out(j, slice(c, c + P))
-        nc.sync.dma_start(out=out_rows[j], in_=y[:, j, :])
+        nc.sync.dma_start(out=out_rows[:, j, :], in_=y[:, j, :])
         for c in range(0, N - P, P):
             interleave(nc.vector.tensor_copy, c, c + P)
         interleave(nc.scalar.copy, N - P, N)

@@ -22,20 +22,27 @@ PACK = 4
 PASS = P * PACK
 PASSES = T // PASS
 TILES = K // P
+QUADRANT = 32
 RUN = 16
 PAD = 8
-OUT_SCALE = 0.03
-HALF = N // 2
 ROWS = T // P
-STEPS = 2 * TILES * PASSES
-LAG = 3
+HALF = N // 2
+OUT_SCALE = 0.03
+
+SET_STEPS = TILES * PASSES
+STEPS = 2 * SET_STEPS
+LAG = 4
+PRODUCT_BUFS = 6
+SPREAD_RA_STEP = 2
+DEAL_SCALE_STEP = 4
+STORED_STEP = 5
 
 
 def tile_mix_lagged_moments_pl_kernel(tc, xa, xb, ra, rb, sa_words, sa_scales, sb_words, sb_scales, out_0, out_1, out_2):
     nc = tc.nc
     with ExitStack() as ctx:
         keep = ctx.enter_context(tc.tile_pool(name="keep", bufs=1))
-        work = ctx.enter_context(tc.tile_pool(name="work", bufs=3))
+        work = ctx.enter_context(tc.tile_pool(name="work", bufs=1))
         psum = ctx.enter_context(tc.psum_pool(name="psum", bufs=1))
         ctx.enter_context(tc.manual_schedule())
 
@@ -53,18 +60,18 @@ def tile_mix_lagged_moments_pl_kernel(tc, xa, xb, ra, rb, sa_words, sa_scales, s
         for b in range(TILES):
             nc.scalar.activation(out=xb_sb[b][:, PAD - 1 : PAD], in_=rows[:, P : P + 1], func=COPY)
 
-        def load_scales(plane, scales, quadrants):
-            for q in quadrants:
+        def load_scales(plane, scales, rs):
+            for r in rs:
                 nc.sync.dma_start(
-                    out=plane[32 * q : 32 * q + 4, :, :].bitcast(I32),
-                    in_=scales[:, 4 * q : 4 * q + 4, :].rearrange("z r c -> r z c").bitcast(I32),
+                    out=plane[r:P:QUADRANT, :, :].bitcast(I32),
+                    in_=scales.rearrange("z (q r) c -> r q z c", r=PACK)[r].bitcast(I32),
                 )
-
-        xa_rows = xa.rearrange("(p j) t -> j p t", j=PACK)
-        out_rows = out_0.rearrange("(p j) n -> p j n", j=PACK)
 
         def load_xb(b):
             nc.sync.dma_start(out=xb_sb[b][:, PAD:], in_=xb[P * b : P * (b + 1), :])
+
+        xa_rows = xa.rearrange("(p j) t -> j p t", j=PACK)
+        out_rows = out_0.rearrange("(p j) n -> p j n", j=PACK)
 
         sa_raw = keep.tile([P, PASSES, 2 * K], U8, align_bytes=64)
         nc.sync.dma_start(out=sa_raw[:].bitcast(I32), in_=sa_words.rearrange("z p c -> p z c").bitcast(I32))
@@ -80,12 +87,13 @@ def tile_mix_lagged_moments_pl_kernel(tc, xa, xb, ra, rb, sa_words, sa_scales, s
         sb_codes = keep.tile([P, PASSES, N], U32, align_bytes=64)
         nc.sync.dma_start(out=sb_codes[:].bitcast(I32), in_=sb_words.rearrange("z p c r -> p z (c r)").bitcast(I32))
         load_scales(sb_scale, sb_scales, (2, 3))
-        xa_sb = [keep.tile([P, T], F32, name="xa_sb%d" % j) for j in range(TILES - 1)]
-        for j in range(TILES - 1):
+        last = TILES - 1
+        xa_sb = [keep.tile([P, T], F32, name="xa_sb%d" % j) for j in range(last)]
+        for j in range(last):
             nc.sync.dma_start(out=xa_sb[j][:], in_=xa_rows[j])
         xa_last = [keep.tile([P, PASS], F32, name="xa_last%d" % z) for z in range(PASSES)]
         for z in range(PASSES):
-            nc.sync.dma_start(out=xa_last[z][:], in_=xa_rows[TILES - 1][:, PASS * z : PASS * (z + 1)])
+            nc.sync.dma_start(out=xa_last[z][:], in_=xa_rows[last][:, PASS * z : PASS * (z + 1)])
 
         rows_turned = psum.tile([P, P], F32, tag="acc2")
         nc.tensor.transpose(rows_turned[:], rows[:, :P], ident[:])
@@ -111,6 +119,9 @@ def tile_mix_lagged_moments_pl_kernel(tc, xa, xb, ra, rb, sa_words, sa_scales, s
         )
         sa_scale = keep.tile([P, PASSES, TILES, P], U8, align_bytes=64)
 
+        def deal_sa_scale():
+            nc.vector.tensor_copy(out=sa_scale[:], in_=sa_scale_raw[:].rearrange("p z (c j) -> p z j c", j=PACK))
+
         tb_codes = [keep.tile([P, N], U32, align_bytes=64, name="tb_codes%d" % z) for z in range(PASSES)]
         tb_scale = [keep.tile([P, N], U8, align_bytes=64, name="tb_scale%d" % z) for z in range(PASSES)]
         ta_codes = [keep.tile([P, PASSES, P], U32, align_bytes=64, name="ta_codes%d" % j) for j in range(TILES)]
@@ -128,9 +139,9 @@ def tile_mix_lagged_moments_pl_kernel(tc, xa, xb, ra, rb, sa_words, sa_scales, s
                 weights = rb_banks[z][:]
             else:
                 j = tile - TILES
-                src = xa_sb[j][:, PASS * z : PASS * (z + 1)] if j < TILES - 1 else xa_last[z][:]
+                src = xa_sb[j][:, PASS * z : PASS * (z + 1)] if j < last else xa_last[z][:]
                 weights = ra_row[:, z, :]
-            prod = work.tile([P, PASS], BF16, align_bytes=64, bufs=6)
+            prod = work.tile([P, PASS], BF16, align_bytes=64, bufs=PRODUCT_BUFS)
             nc.vector.tensor_tensor(
                 out=prod[:].rearrange("p (u g i) -> p g u i", u=2, i=RUN),
                 in0=src.rearrange("p (g u i) -> p g u i", u=2, i=RUN),
@@ -182,7 +193,8 @@ def tile_mix_lagged_moments_pl_kernel(tc, xa, xb, ra, rb, sa_words, sa_scales, s
                     stop=False,
                 )
 
-        def live_product(j, z):
+        def live_product(step):
+            j, z = divmod(step - SET_STEPS, PASSES)
             nc.tensor.matmul_mx(
                 out=acc[j][:],
                 lhsT=ta_codes[j][:, z, :].bitcast(E4M3),
@@ -193,41 +205,34 @@ def tile_mix_lagged_moments_pl_kernel(tc, xa, xb, ra, rb, sa_words, sa_scales, s
                 stop=(z == PASSES - 1),
             )
 
-        def scale_out(j, cols):
-            nc.scalar.activation(out=y[:, j, cols], in_=acc[j][:, cols], func=COPY, scale=OUT_SCALE)
+        def scale_out(j, c0, c1):
+            nc.scalar.activation(out=y[:, j, c0:c1], in_=acc[j][:, c0:c1], func=COPY, scale=OUT_SCALE)
 
-        def store(j):
-            scale_out(j, slice(0, N))
-            if j == 0:
-                nc.sync.dma_start(out=out_rows[:, j, :], in_=y[:, j, :])
+        def store_out(j0, j1):
+            nc.sync.dma_start(out=out_rows[:, j0:j1, :], in_=y[:, j0:j1, :])
 
         for step in range(STEPS):
-            if step == 4:
-                nc.vector.tensor_copy(out=sa_scale[:], in_=sa_scale_raw[:].rearrange("p z (c j) -> p z j c", j=PACK))
+            if step == DEAL_SCALE_STEP:
+                deal_sa_scale()
             prod = weigh(step)
             if step >= LAG:
                 quantise(step - LAG)
             turn(step, prod)
-            done, z = divmod(step - LAG - 1 - STEPS // 2, PASSES)
-            if done >= 0 and z == PASSES - 1:
-                store(done)
-            if step in (2, 3):
-                spread_ra(step - 2)
-            if step in range(5, 5 + 2 * TILES, 2):
-                stored_product((step - 5) // 2)
-            done, z = divmod(step - LAG - STEPS // 2, PASSES)
-            if done >= 0 and z == PASSES - 1:
-                live_product(done, 0)
-                live_product(done, 1)
-        j = TILES - 1
-        quantise(STEPS - 3)
-        live_product(j - 1, 0)
-        live_product(j - 1, 1)
-        for z in range(PASSES):
-            quantise(STEPS - PASSES + z)
-            live_product(j, z)
-        nc.vector.tensor_scalar(out=y[:, j - 1, :], in0=acc[j - 1][:], scalar1=OUT_SCALE, scalar2=None, op0=MULT)
-        nc.sync.dma_start(out=out_rows[:, 1:j, :], in_=y[:, 1:j, :])
+            if step == SET_STEPS + PASSES + LAG:
+                scale_out(0, 0, N)
+                store_out(0, 1)
+            if step in range(SPREAD_RA_STEP, SPREAD_RA_STEP + PASSES):
+                spread_ra(step - SPREAD_RA_STEP)
+            if step in range(STORED_STEP, STORED_STEP + 2 * TILES, 2):
+                stored_product((step - STORED_STEP) // 2)
+            if step - LAG >= SET_STEPS:
+                live_product(step - LAG)
+        scale_out(1, 0, N)
+        for step in range(STEPS - LAG, STEPS):
+            quantise(step)
+            live_product(step)
+        nc.vector.tensor_scalar(out=y[:, 2, :], in0=acc[2][:], scalar1=OUT_SCALE, scalar2=None, op0=MULT)
+        store_out(1, last)
 
         y_grouped = keep.tile([P, N, PACK], BF16, align_bytes=64)
         y_codes = keep.tile([P, N], U32, align_bytes=64)
@@ -239,27 +244,27 @@ def tile_mix_lagged_moments_pl_kernel(tc, xa, xb, ra, rb, sa_words, sa_scales, s
                 in_=y[:, :, c0:c1].rearrange("p j (c i) -> p c j i", i=4),
             )
 
+        words_out = out_1.rearrange("z p c r -> p (z c r)").bitcast(I32)
+
         def quantise_y(c0, c1):
             nc.vector.quantize_mx(
                 out=y_codes[:, c0:c1].bitcast(E4M3),
                 scales=y_scale[:, c0:c1],
                 in_=y_grouped[:, c0:c1, :].rearrange("p c j -> p (c j)"),
             )
+            nc.sync.dma_start(out=words_out[:, c0:c1], in_=y_codes[:, c0:c1].bitcast(I32))
 
         for c in range(0, N, P):
-            scale_out(j, slice(c, c + P))
-        nc.sync.dma_start(out=out_rows[:, j, :], in_=y[:, j, :])
+            scale_out(last, c, c + P)
+        store_out(last, TILES)
         for c in range(0, N - P, P):
             interleave(nc.vector.tensor_copy, c, c + P)
         interleave(nc.scalar.copy, N - P, N)
-        words_out = out_1.rearrange("z p c r -> p (z c r)").bitcast(I32)
         quantise_y(0, HALF)
-        nc.sync.dma_start(out=words_out[:, :HALF], in_=y_codes[:, :HALF].bitcast(I32))
         quantise_y(HALF, N)
-        nc.sync.dma_start(out=words_out[:, HALF:], in_=y_codes[:, HALF:].bitcast(I32))
-        for q in range(4):
-            queue = nc.scalar if q % 2 == 0 else nc.sync
+        for r in range(PACK):
+            queue = nc.scalar if r % 2 == 0 else nc.sync
             queue.dma_start(
-                out=out_2[0, 4 * q : 4 * q + 4, :].bitcast(I32),
-                in_=y_scale[32 * q : 32 * q + 4, :].bitcast(I32),
+                out=out_2[0].rearrange("(q r) c -> r q c", r=PACK)[r].bitcast(I32),
+                in_=y_scale[r:P:QUADRANT, :].bitcast(I32),
             )

from contextlib import ExitStack

import concourse.mybir as mybir
from concourse.masks import make_identity

K, N, T, S = 512, 512, 1024, 1024
FLOPS = 2 * K * N * (T + S)

F32 = mybir.dt.float32
BF16 = mybir.dt.bfloat16
I32 = mybir.dt.int32
U32 = mybir.dt.uint32
U8 = mybir.dt.uint8
E4M3 = mybir.dt.float8_e4m3fn_x4
E5M2 = mybir.dt.float8_e5m2_x4
E2M1 = mybir.dt.float4_e2m1fn_x4
MULT = mybir.AluOpType.mult
COPY = mybir.ActivationFunctionType.Copy

P = 128
PACK = 4
PASS = P * PACK
PASSES = T // PASS
TILES = K // P
QUADRANT = 32
RUN = 16
PAD = 8
ROWS = T // P
HALF = N // 2
OUT_SCALE = 0.03

SET_STEPS = TILES * PASSES
STEPS = 2 * SET_STEPS
LAG = 4
PRODUCT_BUFS = 6
SPREAD_RA_STEP = 2
DEAL_SCALE_STEP = 4
STORED_STEP = 5


def tile_mix_lagged_moments_pl_kernel(tc, xa, xb, ra, rb, sa_words, sa_scales, sb_words, sb_scales, out_0, out_1, out_2):
    nc = tc.nc
    with ExitStack() as ctx:
        keep = ctx.enter_context(tc.tile_pool(name="keep", bufs=1))
        work = ctx.enter_context(tc.tile_pool(name="work", bufs=1))
        psum = ctx.enter_context(tc.psum_pool(name="psum", bufs=1))
        ctx.enter_context(tc.manual_schedule())

        rows = keep.tile([P, P + PAD], F32)
        nc.gpsimd.memset(rows[:], 0.0)
        ident = keep.tile([P, P], F32)
        make_identity(nc, ident[:])

        sa_scale_raw = keep.tile([P, PASSES, K], U8, align_bytes=64)
        sb_scale = keep.tile([P, PASSES, N], U8, align_bytes=64)
        nc.vector.memset(sa_scale_raw[:].rearrange("p z c -> p (z c)").bitcast(I32), 0)
        nc.vector.memset(sb_scale[:].rearrange("p z c -> p (z c)").bitcast(I32), 0)

        xb_sb = [keep.tile([P, PAD + T], F32, name="xb_sb%d" % b) for b in range(TILES)]
        for b in range(TILES):
            nc.scalar.activation(out=xb_sb[b][:, PAD - 1 : PAD], in_=rows[:, P : P + 1], func=COPY)

        def load_scales(plane, scales, rs):
            for r in rs:
                nc.sync.dma_start(
                    out=plane[r:P:QUADRANT, :, :].bitcast(I32),
                    in_=scales.rearrange("z (q r) c -> r q z c", r=PACK)[r].bitcast(I32),
                )

        def load_xb(b):
            nc.sync.dma_start(out=xb_sb[b][:, PAD:], in_=xb[P * b : P * (b + 1), :])

        xa_rows = xa.rearrange("(p j) t -> j p t", j=PACK)
        out_rows = out_0.rearrange("(p j) n -> p j n", j=PACK)

        sa_raw = keep.tile([P, PASSES, 2 * K], U8, align_bytes=64)
        nc.sync.dma_start(out=sa_raw[:].bitcast(I32), in_=sa_words.rearrange("z p c -> p z c").bitcast(I32))
        nc.sync.dma_start(out=rows[0:ROWS, :P], in_=rb.rearrange("o (m n) -> (o m) n", n=P))
        nc.sync.dma_start(out=rows[ROWS : 2 * ROWS, :P], in_=ra.rearrange("o (m n) -> (o m) n", n=P))
        load_xb(0)
        load_xb(1)
        load_scales(sa_scale_raw, sa_scales, (0, 1))
        load_xb(2)
        load_scales(sa_scale_raw, sa_scales, (2, 3))
        load_xb(3)
        load_scales(sb_scale, sb_scales, (0, 1))
        sb_codes = keep.tile([P, PASSES, N], U32, align_bytes=64)
        nc.sync.dma_start(out=sb_codes[:].bitcast(I32), in_=sb_words.rearrange("z p c r -> p z (c r)").bitcast(I32))
        load_scales(sb_scale, sb_scales, (2, 3))
        last = TILES - 1
        xa_sb = [keep.tile([P, T], F32, name="xa_sb%d" % j) for j in range(last)]
        for j in range(last):
            nc.sync.dma_start(out=xa_sb[j][:], in_=xa_rows[j])
        xa_last = [keep.tile([P, PASS], F32, name="xa_last%d" % z) for z in range(PASSES)]
        for z in range(PASSES):
            nc.sync.dma_start(out=xa_last[z][:], in_=xa_rows[last][:, PASS * z : PASS * (z + 1)])

        rows_turned = psum.tile([P, P], F32, tag="acc2")
        nc.tensor.transpose(rows_turned[:], rows[:, :P], ident[:])
        cols = keep.tile([P, 2 * ROWS], F32)
        nc.scalar.copy(out=cols[:], in_=rows_turned[:, : 2 * ROWS])

        def spread(first, tag):
            bank = psum.tile([P, PASS], F32, tag=tag)
            for m in range(PACK):
                nc.tensor.transpose(bank[:, P * m : P * (m + 1)], cols[:, first + m : first + m + 1].to_broadcast([P, P]), ident[:])
            return bank

        rb_banks = [spread(PACK * z, "spare%d" % z) for z in range(PASSES)]
        ra_row = keep.tile([P, PASSES, PASS], F32)

        def spread_ra(z):
            nc.scalar.copy(out=ra_row[:, z, :], in_=spread(ROWS + PACK * z, "acc%d" % (2 + z))[:])

        sa_codes = keep.tile([P, PASSES, TILES, 2 * P], U8, align_bytes=64)
        nc.vector.tensor_copy(
            out=sa_codes[:].rearrange("p z j (c b) -> p z j c b", b=2),
            in_=sa_raw[:].rearrange("p z (c j b) -> p z j c b", j=PACK, b=2),
        )
        sa_scale = keep.tile([P, PASSES, TILES, P], U8, align_bytes=64)

        def deal_sa_scale():
            nc.vector.tensor_copy(out=sa_scale[:], in_=sa_scale_raw[:].rearrange("p z (c j) -> p z j c", j=PACK))

        tb_codes = [keep.tile([P, N], U32, align_bytes=64, name="tb_codes%d" % z) for z in range(PASSES)]
        tb_scale = [keep.tile([P, N], U8, align_bytes=64, name="tb_scale%d" % z) for z in range(PASSES)]
        ta_codes = [keep.tile([P, PASSES, P], U32, align_bytes=64, name="ta_codes%d" % j) for j in range(TILES)]
        ta_scale = [keep.tile([P, PASSES, P], U8, align_bytes=64, name="ta_scale%d" % j) for j in range(TILES)]
        y = keep.tile([P, TILES, N], F32, align_bytes=64)
        acc = {}

        tb_grouped = [keep.tile([P, 2 * P, PACK], BF16, align_bytes=64, name="tb_grouped%d" % i) for i in range(2 * PASSES)]
        ta_grouped = {}

        def weigh(step):
            tile, z = divmod(step, PASSES)
            if tile < TILES:
                src = xb_sb[tile][:, PAD - 1 + PASS * z : PAD - 1 + PASS * (z + 1)]
                weights = rb_banks[z][:]
            else:
                j = tile - TILES
                src = xa_sb[j][:, PASS * z : PASS * (z + 1)] if j < last else xa_last[z][:]
                weights = ra_row[:, z, :]
            prod = work.tile([P, PASS], BF16, align_bytes=64, bufs=PRODUCT_BUFS)
            nc.vector.tensor_tensor(
                out=prod[:].rearrange("p (u g i) -> p g u i", u=2, i=RUN),
                in0=src.rearrange("p (g u i) -> p g u i", u=2, i=RUN),
                in1=weights.rearrange("p (g u i) -> p g u i", u=2, i=RUN),
                op=MULT,
            )
            return prod

        def turn(step, prod):
            tile, z = divmod(step, PASSES)
            tags = ("turn0", "turn1") if tile < TILES else ("spare0", "spare1", "turn0", "turn1")
            bank = psum.tile([P, 2, P], F32, tag=tags[step % len(tags)])
            for u in range(2):
                nc.tensor.transpose(bank[:, u, :], prod[:].bitcast(F32)[:, P * u : P * (u + 1)], ident[:])
            if tile < TILES:
                grouped = tb_grouped[PASSES * (tile // 2) + z][:, P * (tile % 2) : P * (tile % 2 + 1), :]
            else:
                ta_tile = work.tile([P, P, PACK], BF16, align_bytes=64, bufs=LAG + 2)
                ta_grouped[step] = ta_tile
                grouped = ta_tile[:]
            nc.scalar.copy(out=grouped.bitcast(F32), in_=bank[:].rearrange("p u c -> p c u"))

        def quantise(step):
            tile, z = divmod(step, PASSES)
            if tile >= TILES:
                nc.vector.quantize_mx(
                    out=ta_codes[tile - TILES][:, z, :].bitcast(E4M3),
                    scales=ta_scale[tile - TILES][:, z, :],
                    in_=ta_grouped[step][:].rearrange("p c r -> p (c r)"),
                )
            elif tile % 2 == 1:
                half = slice(HALF * (tile // 2), HALF * (tile // 2 + 1))
                nc.vector.quantize_mx(
                    out=tb_codes[z][:, half].bitcast(E5M2),
                    scales=tb_scale[z][:, half],
                    in_=tb_grouped[PASSES * (tile // 2) + z][:].rearrange("p c r -> p (c r)"),
                )

        def stored_product(j):
            acc[j] = psum.tile([P, N], F32, tag="acc%d" % j, name="acc%d" % j)
            for z in range(PASSES):
                nc.tensor.matmul_mx(
                    out=acc[j][:],
                    lhsT=sa_codes[:, z, j, :].bitcast(E2M1),
                    lhsT_scale=sa_scale[:, z, j, :],
                    rhs=sb_codes[:, z, :].bitcast(E4M3),
                    rhs_scale=sb_scale[:, z, :],
                    start=(z == 0),
                    stop=False,
                )

        def live_product(step):
            j, z = divmod(step - SET_STEPS, PASSES)
            nc.tensor.matmul_mx(
                out=acc[j][:],
                lhsT=ta_codes[j][:, z, :].bitcast(E4M3),
                lhsT_scale=ta_scale[j][:, z, :],
                rhs=tb_codes[z][:].bitcast(E5M2),
                rhs_scale=tb_scale[z][:],
                start=False,
                stop=(z == PASSES - 1),
            )

        def scale_out(j, c0, c1):
            nc.scalar.activation(out=y[:, j, c0:c1], in_=acc[j][:, c0:c1], func=COPY, scale=OUT_SCALE)

        def store_out(j0, j1):
            nc.sync.dma_start(out=out_rows[:, j0:j1, :], in_=y[:, j0:j1, :])

        for step in range(STEPS):
            if step == DEAL_SCALE_STEP:
                deal_sa_scale()
            prod = weigh(step)
            if step >= LAG:
                quantise(step - LAG)
            turn(step, prod)
            if step == SET_STEPS + PASSES + LAG:
                scale_out(0, 0, N)
                store_out(0, 1)
            if step in range(SPREAD_RA_STEP, SPREAD_RA_STEP + PASSES):
                spread_ra(step - SPREAD_RA_STEP)
            if step in range(STORED_STEP, STORED_STEP + 2 * TILES, 2):
                stored_product((step - STORED_STEP) // 2)
            if step - LAG >= SET_STEPS:
                live_product(step - LAG)
        scale_out(1, 0, N)
        for step in range(STEPS - LAG, STEPS):
            quantise(step)
            live_product(step)
        nc.vector.tensor_scalar(out=y[:, 2, :], in0=acc[2][:], scalar1=OUT_SCALE, scalar2=None, op0=MULT)
        store_out(1, last)

        y_grouped = keep.tile([P, N, PACK], BF16, align_bytes=64)
        y_codes = keep.tile([P, N], U32, align_bytes=64)
        y_scale = keep.tile([P, N], U8, align_bytes=64)

        def interleave(copy, c0, c1):
            copy(
                out=y_grouped[:, c0:c1, :].rearrange("p (c i) j -> p c j i", i=4),
                in_=y[:, :, c0:c1].rearrange("p j (c i) -> p c j i", i=4),
            )

        words_out = out_1.rearrange("z p c r -> p (z c r)").bitcast(I32)

        def quantise_y(c0, c1):
            nc.vector.quantize_mx(
                out=y_codes[:, c0:c1].bitcast(E4M3),
                scales=y_scale[:, c0:c1],
                in_=y_grouped[:, c0:c1, :].rearrange("p c j -> p (c j)"),
            )
            nc.sync.dma_start(out=words_out[:, c0:c1], in_=y_codes[:, c0:c1].bitcast(I32))

        for c in range(0, N, P):
            scale_out(last, c, c + P)
        store_out(last, TILES)
        for c in range(0, N - P, P):
            interleave(nc.vector.tensor_copy, c, c + P)
        interleave(nc.scalar.copy, N - P, N)
        quantise_y(0, HALF)
        quantise_y(HALF, N)
        for r in range(PACK):
            queue = nc.scalar if r % 2 == 0 else nc.sync
            queue.dma_start(
                out=out_2[0].rearrange("(q r) c -> r q c", r=PACK)[r].bitcast(I32),
                in_=y_scale[r:P:QUADRANT, :].bitcast(I32),
            )
